import numpy as np
import ml_dtypes


def mxq(x, axis, fmt="e4m3"):
    dtype, down = {"e4m3": (ml_dtypes.float8_e4m3fn, 7), "e5m2": (ml_dtypes.float8_e5m2, 14)}[fmt]
    v = np.moveaxis(np.asarray(x, np.float32).astype(ml_dtypes.bfloat16).astype(np.float64), axis, -1)
    blocks = v.reshape(v.shape[:-1] + (-1, 32))
    amax = np.abs(blocks).max(-1, keepdims=True)
    byte = np.maximum(np.where(amax > 0, np.frexp(amax)[1] - 1 + 127, 0) - down, 1)
    scale = np.exp2(byte - 127.0)
    codes = (blocks / scale).astype(np.float32).astype(dtype).astype(np.float64)
    return np.moveaxis((codes * scale).reshape(v.shape), -1, axis)


WIDE = False


def mx_kscale(k):
    if not WIDE:
        return np.ones(k)
    levels = np.array([10, -10, 5, -5, 0])
    if k % 512:
        return np.exp2(np.random.permutation(np.resize(levels, k // 32))).repeat(32)
    a = np.empty((k // 512, 16))
    for p in range(k // 512):
        a[p, :8] = np.random.permutation(np.resize(levels, 8))
        for g in range(8):
            far = levels[np.abs(levels - a[p, g]) >= 10]
            a[p, g + 8] = far[np.random.randint(len(far))]
    return np.exp2(a.ravel()).repeat(32)


def f64(x):
    return np.asarray(x).astype(np.float64)


def striped(idx):
    return np.tile(idx.reshape(-1, 16).T, (8, 1)).astype(np.uint16)


def unstriped(offs):
    return offs[:16].T.reshape(-1).astype(np.int64)


E2M1 = np.array([0.0, 0.5, 1.0, 1.5, 2.0, 3.0, 4.0, 6.0, -0.0, -0.5, -1.0, -1.5, -2.0, -3.0, -4.0, -6.0])


def pack_weight(w, fmt):
    k, n = w.shape
    w = f64(np.asarray(w, np.float32).astype(ml_dtypes.bfloat16)).reshape(k // 32, 32, n)
    amax = np.abs(w).max(1)
    if fmt == "e4m3":
        byte = np.frexp(amax)[1] - 1 + 127 - 7
    else:
        mant, ex = np.frexp(amax / 6.0)
        byte = np.where(mant > 0.5, ex, ex - 1) + 127
    byte = np.clip(np.where(amax > 0, byte, 1), 1, 254)
    scaled = (w * np.exp2(127.0 - byte)[:, None, :]).reshape(k, n).astype(np.float32)
    by_word = np.ascontiguousarray(scaled.reshape(k // 512, 128, 4, n).transpose(0, 1, 3, 2))
    if fmt == "e4m3":
        words = by_word.astype(ml_dtypes.float8_e4m3fn).view(np.uint8)
    else:
        c = by_word.astype(ml_dtypes.float4_e2m1fn).view(np.uint8) & 0xF
        words = (c[..., 0::2] | (c[..., 1::2] << 4)).reshape(k // 512, 128, 2 * n)
    return np.ascontiguousarray(words), np.ascontiguousarray(byte.astype(np.uint8).reshape(k // 512, 16, n))


def unpack_weight(words, scales, fmt):
    g, _, n = scales.shape
    words = np.ascontiguousarray(words).reshape(g, 128, n, -1)
    if fmt == "e4m3":
        vals = words.view(ml_dtypes.float8_e4m3fn).astype(np.float64)
    else:
        nib = np.empty((g, 128, n, 4), np.uint8)
        nib[..., 0::2] = words & 0xF
        nib[..., 1::2] = words >> 4
        vals = E2M1[nib]
    vals = vals * np.repeat(np.exp2(scales.astype(np.float64) - 127.0), 8, axis=1)[..., None]
    return vals.transpose(0, 1, 3, 2).reshape(g * 512, n)


def gelu(v):
    return 0.5 * v * (1.0 + np.tanh(np.sqrt(2.0 / np.pi) * (v + 0.044715 * v**3)))


K, H, T, S, T2, P = 1536, 512, 4096, 1024, 2048, 1024

def setup_inputs():
    n = np.random.standard_normal
    s = mx_kscale(K)[:, None]
    u = mx_kscale(H)[:, None]
    d = {}
    d["tab_words"], d["tab_scales"] = pack_weight(n((K, T)) * s, "e4m3")
    d["offs"] = striped(np.random.permutation(T)[:S])
    d["offs2"] = striped(np.random.permutation(T2)[:S])
    d["offs3"] = striped(np.random.permutation(T2)[:P])
    d["offs4"] = striped(np.random.permutation(T2)[:P])
    d["w1"] = (0.6 * n((K, H)) / K**0.5 / s * u.T).astype(np.float32)
    d["w2_words"], d["w2_scales"] = pack_weight(0.54 * n((K, H)) / K**0.5 / s, "e2m1")
    d["gs"] = (np.random.uniform(1.9, 2.9, H) * u[:, 0]).astype(np.float32)
    d["wgs"] = np.exp(0.3 * n((128, S))).astype(np.float32)
    d["page0"] = (n((H, T2)) * u).astype(np.float32)
    d["sc"] = (np.exp(0.4 * n(H)) / u[:, 0]).astype(np.float32)
    d["gt"] = (np.exp(0.4 * n(H)) * u[:, 0]).astype(np.float32)
    d["w3"] = (1.1 * n((H, H)) / H**0.5 / u).astype(np.float32)
    d["w4_words"], d["w4_scales"] = pack_weight(0.8 * n((H, H)) / H**0.5 / u, "e4m3")
    d["gv"] = (np.exp(0.4 * n(H)) / u[:, 0]).astype(np.float32)
    return d

def reference(tab_words, tab_scales, offs, offs2, offs3, offs4, w1, w2_words, w2_scales, gs, wgs, page0, sc, gt, w3, w4_words, w4_scales, gv):
    v = unpack_weight(tab_words, tab_scales, "e4m3")[:, unstriped(offs)]
    a = mxq(f64(w1), 0, "e4m3").T @ v
    b = unpack_weight(w2_words, w2_scales, "e2m1").T @ v
    h = a + f64(gs)[:, None] * np.sin(b)
    page = f64(page0).copy()
    page[:, unstriped(offs2)] = np.tile(f64(wgs), (H // 128, 1)) * h
    x = page[:, unstriped(offs3)]
    t = mxq(f64(gt)[:, None] * np.tanh(f64(sc)[:, None] * x), 0, "e4m3")
    e = mxq(np.abs(x), 0, "e4m3")
    y1 = mxq(f64(w3), 0, "e4m3").T @ t
    y2 = unpack_weight(w4_words, w4_scales, "e4m3").T @ e
    variants = page[:, unstriped(offs4)]
    return y1 - y2 + f64(gv)[:, None] * variants

@@ -1,0 +1,344 @@
+import math
+from contextlib import ExitStack
+
+import concourse.mybir as mybir
+from concourse.masks import make_identity
+
+K, H, T, S, T2, M = 1536, 512, 4096, 1024, 2048, 1024
+FLOPS = 2 * (2 * K * H * S) + 2 * (2 * H * H * M)
+
+F32 = mybir.dt.float32
+BF16 = mybir.dt.bfloat16
+I32 = mybir.dt.int32
+U32 = mybir.dt.uint32
+U16 = mybir.dt.uint16
+U8 = mybir.dt.uint8
+FP8X4 = mybir.dt.float8_e4m3fn_x4
+FP4X4 = mybir.dt.float4_e2m1fn_x4
+ALU = mybir.AluOpType
+ACT = mybir.ActivationFunctionType
+
+P = 128
+PACK = 4
+PASSES = K // (P * PACK)
+BANK = 512
+BANK_BYTES = 4 * BANK
+HALVES = S // BANK
+BLOCKS = BANK // P
+CHUNK = 256
+CHUNKS = M // CHUNK
+QUADS = 4
+TWO_PI = 2.0 * math.pi
+ROUNDER = 1.5 * 2.0**23
+KIB = 1024
+
+
+def tile_list_handshape_page_features_kernel(
+    tc, tab_words, tab_scales, offs, offs2, offs3, offs4, w1, w2_words, w2_scales, gs, wgs, page0, sc, gt, w3,
+    w4_words, w4_scales, gv, out,
+):
+    nc = tc.nc
+    with ExitStack() as ctx:
+        lists = ctx.enter_context(tc.tile_pool(name="lists", bufs=1))
+        keep = ctx.enter_context(tc.tile_pool(name="keep", bufs=1))
+        shared = ctx.enter_context(tc.tile_pool(name="shared", bufs=1))
+        ring = ctx.enter_context(tc.tile_pool(name="ring", bufs=2))
+        psum = ctx.enter_context(tc.psum_pool(name="psum", bufs=1))
+
+        def part_of_list(tile, part, width):
+            cols = width // 16
+            return tile[:, part * cols : (part + 1) * cols]
+
+        def span(part, width):
+            return slice(part * width, (part + 1) * width)
+
+        def bank_tile(name, bank):
+            return psum.tile([P, BANK], F32, name=name, offset=bank * BANK_BYTES)
+
+        idx = lists.tile([P, S // 16], U16, name="idx")
+        idx2 = lists.tile([P, S // 16], U16, name="idx2")
+        idx3 = lists.tile([P, M // 16], U16, name="idx3")
+        idx4 = lists.tile([P, M // 16], U16, name="idx4")
+
+        tab = [shared.tile([P, T], I32, name=f"tab{a}", offset=16 * KIB * a) for a in range(PASSES)]
+        w1_raw = [shared.tile([P, PACK, H], F32, name=f"w1_raw{a}", offset=48 * KIB + 8 * KIB * a) for a in range(PASSES)]
+
+        tab_sc = keep.tile([P, T], U8, name="tab_sc")
+        v_sc = [keep.tile([P, S], U8, name=f"v_sc{a}", align_bytes=64) for a in range(PASSES)]
+        w2_codes = keep.tile([P, PASSES, 2 * H], U8, name="w2_codes", align_bytes=64)
+        w2_sc = keep.tile([P, PASSES, H], U8, name="w2_sc", align_bytes=64)
+        w4_sc = keep.tile([P, H], U8, name="w4_sc", align_bytes=64)
+        for tile in (tab_sc[:], w2_sc[:].rearrange("p a c -> p (a c)"), v_sc[1][:], v_sc[2][:], w4_sc[:]):
+            nc.vector.memset(tile.bitcast(I32), 0)
+        ident = keep.tile([P, P], F32, name="ident")
+        make_identity(nc, ident[:])
+        warm = keep.tile([P, 1], F32, name="warm")
+        nc.scalar.activation(warm[:], ident[:, 0:1], ACT.Silu)
+
+        nc.sync.dma_start(idx[:], offs)
+
+        def load_tab(a):
+            nc.sync.dma_start(tab[a][:], tab_words[a].rearrange("p t i -> p (t i)").bitcast(I32))
+
+        for q in range(QUADS):
+            nc.gpsimd.dma_start(
+                tab_sc[32 * q : 32 * q + 4 * PASSES, :].bitcast(I32),
+                tab_scales[:, 4 * q : 4 * q + 4, :].bitcast(I32),
+            )
+        load_tab(0)
+        nc.sync.dma_start(w2_codes[:].bitcast(I32), w2_words.rearrange("a p c -> p a c").bitcast(I32))
+        load_tab(1)
+        for q in range(QUADS):
+            nc.gpsimd.dma_start(
+                w2_sc[32 * q : 32 * q + 4, :, :].bitcast(I32),
+                w2_scales[:, 4 * q : 4 * q + 4, :].rearrange("a r c -> r a c").bitcast(I32),
+            )
+        load_tab(2)
+        for a in range(PASSES):
+            nc.sync.dma_start(w1_raw[a][:], w1[a * 512 : (a + 1) * 512, :].rearrange("(p j) c -> p j c", j=PACK))
+
+        rowvec = {}
+
+        def load_rowvec(name, vec):
+            rowvec[name] = keep.tile([P, PACK], F32, name=name)
+            nc.sync.dma_start(rowvec[name][:], vec.rearrange("(p t) -> p t", t=PACK))
+
+        page = [keep.tile([P, T2], F32, name=f"page{t}") for t in range(PACK)]
+        page_rows = page0.rearrange("(p t) c -> t p c", t=PACK)
+        gain_rows = wgs.rearrange("(m t) j -> m t j", t=PACK)
+        gain = {}
+
+        def load_gain(t0, t1, hf, offset):
+            tile = shared.tile([P, t1 - t0, BANK], F32, name=f"gain{t0}{hf}", offset=offset)
+            for q in range(QUADS):
+                nc.sync.dma_start(tile[32 * q : 32 * (q + 1), :, :], gain_rows[:, t0:t1, span(hf, BANK)])
+            for t in range(t0, t1):
+                gain[t, hf] = tile[:, t - t0, :]
+
+        nc.sync.dma_start(idx2[:], offs2)
+        load_rowvec("gs", gs)
+        nc.sync.dma_start(page[0][:], page_rows[0])
+        load_gain(0, 1, 0, 72 * KIB)
+        nc.sync.dma_start(page[1][:], page_rows[1])
+        load_gain(1, PACK, 0, 74 * KIB)
+        nc.sync.dma_start(page[2][:], page_rows[2])
+        nc.sync.dma_start(page[3][:], page_rows[3])
+        load_gain(0, PACK, 1, 80 * KIB)
+        nc.sync.dma_start(idx3[:], offs3)
+        load_rowvec("sc", sc)
+        load_rowvec("gt", gt)
+        w3_raw = shared.tile([P, PACK, H], F32, name="w3_raw", offset=48 * KIB)
+        nc.sync.dma_start(w3_raw[:], w3.rearrange("(p j) c -> p j c", j=PACK))
+        w4_codes = keep.tile([P, H], I32, name="w4_codes", align_bytes=64)
+        nc.sync.dma_start(w4_codes[:], w4_words[0].rearrange("p c i -> p (c i)").bitcast(I32))
+        for q in range(QUADS):
+            nc.sync.dma_start(
+                w4_sc[32 * q : 32 * q + 4, :].bitcast(I32), w4_scales[0, 4 * q : 4 * q + 4, :].bitcast(I32)
+            )
+        nc.sync.dma_start(idx4[:], offs4)
+        load_rowvec("gv", gv)
+
+        nc.vector.tensor_copy(v_sc[0][:], tab_sc[:].indirect(idx[:]))
+        for a in range(1, PASSES):
+            nc.scalar.dma_start(v_sc[a][0:112, :].bitcast(I32), v_sc[0][4 * a : 4 * a + 112, :].bitcast(I32))
+
+        v = [keep.tile([P, S], U32, name=f"v{a}", align_bytes=64) for a in range(PASSES)]
+        b_acc = [bank_tile(f"b_acc{jb}", jb) for jb in range(S // P)]
+        for a in range(PASSES):
+            for hf in range(HALVES):
+                nc.vector.tensor_copy(v[a][:, span(hf, BANK)], tab[a][:].bitcast(U32).indirect(part_of_list(idx, hf, BANK)))
+                for jb in range(hf * BLOCKS, (hf + 1) * BLOCKS):
+                    nc.tensor.matmul_mx(
+                        out=b_acc[jb][:],
+                        lhsT=v[a][:, span(jb, P)].bitcast(FP8X4),
+                        lhsT_scale=v_sc[a][:, span(jb, P)],
+                        rhs=w2_codes[:, a, :].bitcast(FP4X4),
+                        rhs_scale=w2_sc[:, a, :],
+                        start=(a == 0),
+                        stop=(a == PASSES - 1),
+                    )
+
+        def by_slot(acc):
+            return acc[:].rearrange("p (m t) -> p t m", t=PACK)
+
+        turns, whole = {}, {}
+
+        def split_turns(jb):
+            hf, i = divmod(jb, BLOCKS)
+            at = [8 * KIB * ((k + hf) % 3) + 2 * KIB * i for k in range(3)]
+            rounded = shared.tile([P, PACK, P], U32, name=f"rounded{jb}", offset=at[0])
+            nc.scalar.activation(rounded[:], by_slot(b_acc[jb]), ACT.Copy, bias=ROUNDER, scale=1.0 / TWO_PI)
+            turns[jb] = shared.tile([P, PACK, P], F32, name=f"turns{jb}", offset=at[1])
+            nc.scalar.activation(turns[jb][:], by_slot(b_acc[jb]), ACT.Copy, scale=1.0 / TWO_PI)
+            whole[jb] = shared.tile([P, PACK, P], F32, name=f"whole{jb}", offset=at[2])
+            nc.scalar.activation(whole[jb][:], rounded[:], ACT.Copy, bias=ROUNDER, scale=-1.0)
+
+        def transpose_add(acc, first, second):
+            nc.tensor.matmul(acc, first, ident[:], is_transpose=True, start=True, stop=False)
+            nc.tensor.matmul(acc, second, ident[:], is_transpose=True, start=False, stop=True)
+
+        sine = {}
+
+        def sine_of(t, hf):
+            frac = bank_tile(f"frac{t}{hf}", 4 * hf + 2 + t % 2)
+            for i in range(BLOCKS):
+                jb = hf * BLOCKS + i
+                transpose_add(frac[:, span(i, P)], turns[jb][:, t, :], whole[jb][:, t, :])
+            sine[t, hf] = keep.tile([P, BANK], F32, name=f"sine{t}{hf}")
+            nc.scalar.activation(sine[t, hf][:], frac[:], ACT.Sin, scale=TWO_PI)
+
+        def quantize_weight(grouped, name):
+            codes = keep.tile([P, H], U32, name=name + "_codes", align_bytes=64)
+            scales = keep.tile([P, H], U8, name=name + "_sc", align_bytes=64)
+            nc.vector.quantize_mx(out=codes[:].bitcast(FP8X4), scales=scales[:], in_=grouped[:])
+            return codes, scales
+
+        w1_q = []
+        for a in range(PASSES):
+            grouped = ring.tile([P, PACK * H], BF16, name="grouped", align_bytes=64)
+            nc.vector.tensor_copy(
+                grouped[:].rearrange("p (t m j) -> p m j t", t=PACK, j=PACK),
+                w1_raw[a][:].rearrange("p j (m t) -> p m j t", t=PACK),
+            )
+            w1_q.append(quantize_weight(grouped, f"w1_{a}"))
+
+        a_acc, entries = {}, {}
+
+        def multiply_w1(t, hf):
+            acc = bank_tile(f"a_acc{t}{hf}", 4 * hf + t % 2)
+            for a in range(PASSES):
+                nc.tensor.matmul_mx(
+                    out=acc[:],
+                    lhsT=w1_q[a][0][:, span(t, P)].bitcast(FP8X4),
+                    lhsT_scale=w1_q[a][1][:, span(t, P)],
+                    rhs=v[a][:, span(hf, BANK)].bitcast(FP8X4),
+                    rhs_scale=v_sc[0][4 * a : P, span(hf, BANK)],
+                    start=(a == 0),
+                    stop=(a == PASSES - 1),
+                )
+            a_acc[t, hf] = acc
+
+        def make_entries(t, hf):
+            entries[t, hf] = ring.tile([P, BANK], F32, name="entries", bufs=3)
+            nc.vector.scalar_tensor_tensor(
+                entries[t, hf][:], sine[t, hf][:], rowvec["gs"][:, t : t + 1], a_acc[t, hf][:], ALU.mult, ALU.add
+            )
+            if t + 2 < PACK:
+                multiply_w1(t + 2, hf)
+
+        def put_entries(t, hf):
+            nc.vector.tensor_tensor(
+                page[t][:].indirect(part_of_list(idx2, hf, BANK)), entries[t, hf][:], gain[t, hf], ALU.mult
+            )
+
+        x = [shared.tile([P, 2, M], F32, name=f"x{u}", offset=32 * KIB + 8 * KIB * u) for u in range(2)]
+        t_in = [shared.tile([P, CHUNK, PACK], BF16, name=f"t_in{c}", offset=4 * KIB * c, align_bytes=64) for c in range(CHUNKS)]
+        e_in = [shared.tile([P, CHUNK, PACK], BF16, name=f"e_in{c}", offset=4 * KIB * c + 2 * KIB, align_bytes=64) for c in range(CHUNKS)]
+
+        def reread(t, width):
+            for part in range(M // width):
+                nc.vector.tensor_copy(x[t // 2][:, t % 2, span(part, width)], page[t][:].indirect(part_of_list(idx3, part, width)))
+
+        def readings(t, c):
+            cols = span(c, CHUNK)
+            if t % 2 == 1:
+                nc.scalar.activation(e_in[c][:, :, t - 1 : t + 1], x[t // 2][:, :, cols].rearrange("p u m -> p m u"), ACT.Abs)
+            bounded = ring.tile([P, CHUNK], F32, name="bounded")
+            nc.scalar.activation(bounded[:], x[t // 2][:, t % 2, cols], ACT.Tanh, scale=rowvec["sc"][:, t : t + 1])
+            nc.scalar.activation(t_in[c][:, :, t], bounded[:], ACT.Copy, scale=rowvec["gt"][:, t : t + 1])
+
+        for hf in range(HALVES):
+            for jb in range(hf * BLOCKS, (hf + 1) * BLOCKS):
+                split_turns(jb)
+            multiply_w1(0, hf)
+            multiply_w1(1, hf)
+            for t in range(PACK):
+                sine_of(t, hf)
+        w3_grouped = ring.tile([P, PACK * H], BF16, name="grouped", align_bytes=64)
+        nc.scalar.copy(
+            w3_grouped[:].rearrange("p (c i j) -> p c j i", i=PACK, j=PACK),
+            w3_raw[:].rearrange("p j (c i) -> p c j i", i=PACK),
+        )
+
+        steps = [(t, hf) for hf in range(HALVES) for t in range(PACK)]
+        make_entries(*steps[0])
+        for i, (t, hf) in enumerate(steps):
+            if i + 1 < len(steps):
+                make_entries(*steps[i + 1])
+            else:
+                w3_codes, w3_sc = quantize_weight(w3_grouped, "w3")
+            put_entries(t, hf)
+            if hf == HALVES - 1 and t < PACK - 1:
+                reread(t, M)
+                for c in range(CHUNKS):
+                    readings(t, c)
+        reread(PACK - 1, CHUNK)
+        for c in range(CHUNKS):
+            readings(PACK - 1, c)
+
+        out_rows = out.rearrange("(p t) m -> p t m", t=PACK)
+        variants, staged, sums = {}, {}, {}
+
+        def fetch_variants(c):
+            offset = 80 * KIB if c == 0 else 4 * KIB * (c - 1)
+            variants[c] = shared.tile([P, PACK, CHUNK], F32, name=f"variants{c}", offset=offset)
+            for t in range(PACK):
+                nc.vector.tensor_copy(variants[c][:, t, :], page[t][:].indirect(part_of_list(idx4, c, CHUNK)))
+
+        quantized = {}
+
+        def quantize_readings(c):
+            for name, src in (("t", t_in[c]), ("e", e_in[c])):
+                codes = ring.tile([P, CHUNK], U32, name=name + "_codes", align_bytes=64)
+                scales = ring.tile([P, CHUNK], U8, name=name + "_sc", align_bytes=64)
+                nc.vector.quantize_mx(out=codes[:].bitcast(FP8X4), scales=scales[:], in_=src[:].rearrange("p m t -> p (m t)"))
+                quantized[c, name] = (codes, scales)
+
+        def multiply_block(mb):
+            c, i = divmod(mb, CHUNK // P)
+            for which, (name, w_codes, w_sc, sign) in enumerate((("t", w3_codes, w3_sc, 1.0), ("e", w4_codes, w4_sc, -1.0))):
+                codes, scales = quantized[c, name]
+                acc = bank_tile(f"y{mb}{name}", 2 * (mb % 2) + which)
+                nc.tensor.matmul_mx(
+                    out=acc[:],
+                    lhsT=codes[:, span(i, P)].bitcast(FP8X4),
+                    lhsT_scale=scales[:, span(i, P)],
+                    rhs=w_codes[:].bitcast(FP8X4),
+                    rhs_scale=w_sc[:],
+                    start=True,
+                    stop=True,
+                )
+                staged[mb, name] = shared.tile([P, PACK, P], F32, name=f"staged{mb}{name}", offset=(56 + 2 * (2 * (mb % 4) + which)) * KIB)
+                nc.scalar.activation(staged[mb, name][:], by_slot(acc), ACT.Copy, scale=sign)
+
+        def turn_back(mb):
+            c, i = divmod(mb, CHUNK // P)
+            if i == 0:
+                for u in range(2):
+                    sums[c, u] = psum.tile([P, 2, CHUNK], F32, name=f"sums{c}{u}", offset=(4 + 2 * (c % 2) + u) * BANK_BYTES)
+            for t in range(PACK):
+                transpose_add(sums[c, t // 2][:, t % 2, span(i, P)], staged[mb, "t"][:, t, :], staged[mb, "e"][:, t, :])
+
+        def finish(c):
+            for u in range(2):
+                result = shared.tile([P, 2, CHUNK], F32, name=f"result{c}{u}", offset=16 * KIB + 2 * KIB * (2 * c + u))
+                for t in range(2 * u, 2 * u + 2):
+                    nc.vector.scalar_tensor_tensor(
+                        result[:, t % 2, :], variants[c][:, t, :], rowvec["gv"][:, t : t + 1], sums[c, u][:, t % 2, :], ALU.mult, ALU.add
+                    )
+                nc.sync.dma_start(out_rows[:, 2 * u : 2 * u + 2, span(c, CHUNK)], result[:])
+
+        blocks = M // P
+        for mb in range(blocks + 2):
+            c, i = divmod(mb, CHUNK // P)
+            if mb < blocks:
+                if i == 0:
+                    fetch_variants(c)
+                    quantize_readings(c)
+                multiply_block(mb)
+            if i == 0 and c >= 3:
+                finish(c - 3)
+            if mb >= 2:
+                turn_back(mb - 2)
+        finish(CHUNKS - 2)
+        finish(CHUNKS - 1)

@@ -25,7 +25,7 @@ BANK = 512
 BANK_BYTES = 4 * BANK
 HALVES = S // BANK
 BLOCKS = BANK // P
-CHUNK = 256
+CHUNK = 512
 CHUNKS = M // CHUNK
 QUADS = 4
 TWO_PI = 2.0 * math.pi
@@ -67,41 +67,55 @@ def tile_list_handshape_page_features_kernel(
         v_sc = [keep.tile([P, S], U8, name=f"v_sc{a}", align_bytes=64) for a in range(PASSES)]
         w2_codes = keep.tile([P, PASSES, 2 * H], U8, name="w2_codes", align_bytes=64)
         w2_sc = keep.tile([P, PASSES, H], U8, name="w2_sc", align_bytes=64)
-        w4_sc = keep.tile([P, H], U8, name="w4_sc", align_bytes=64)
-        for tile in (tab_sc[:], w2_sc[:].rearrange("p a c -> p (a c)"), v_sc[1][:], v_sc[2][:], w4_sc[:]):
+        w4_sc_raw = keep.tile([P, H], U8, name="w4_sc_raw")
+        for tile in (tab_sc[:], w2_sc[:].rearrange("p a c -> p (a c)"), v_sc[1][:], v_sc[2][:], w4_sc_raw[:]):
             nc.vector.memset(tile.bitcast(I32), 0)
         ident = keep.tile([P, P], F32, name="ident")
         make_identity(nc, ident[:])
         warm = keep.tile([P, 1], F32, name="warm")
         nc.scalar.activation(warm[:], ident[:, 0:1], ACT.Silu)
 
-        nc.sync.dma_start(idx[:], offs)
-
-        def load_tab(a):
-            nc.sync.dma_start(tab[a][:], tab_words[a].rearrange("p t i -> p (t i)").bitcast(I32))
-
-        for q in range(QUADS):
-            nc.gpsimd.dma_start(
-                tab_sc[32 * q : 32 * q + 4 * PASSES, :].bitcast(I32),
-                tab_scales[:, 4 * q : 4 * q + 4, :].bitcast(I32),
-            )
-        load_tab(0)
-        nc.sync.dma_start(w2_codes[:].bitcast(I32), w2_words.rearrange("a p c -> p a c").bitcast(I32))
-        load_tab(1)
-        for q in range(QUADS):
-            nc.gpsimd.dma_start(
-                w2_sc[32 * q : 32 * q + 4, :, :].bitcast(I32),
-                w2_scales[:, 4 * q : 4 * q + 4, :].rearrange("a r c -> r a c").bitcast(I32),
-            )
-        load_tab(2)
-        for a in range(PASSES):
-            nc.sync.dma_start(w1_raw[a][:], w1[a * 512 : (a + 1) * 512, :].rearrange("(p j) c -> p j c", j=PACK))
-
         rowvec = {}
 
         def load_rowvec(name, vec):
             rowvec[name] = keep.tile([P, PACK], F32, name=name)
             nc.sync.dma_start(rowvec[name][:], vec.rearrange("(p t) -> p t", t=PACK))
+
+        def load_tab(a):
+            nc.sync.dma_start(tab[a][:], tab_words[a].rearrange("p t i -> p (t i)").bitcast(I32))
+
+        for tile, src in ((idx, offs), (idx2, offs2), (idx3, offs3), (idx4, offs4)):
+            nc.sync.dma_start(tile[:], src)
+        load_rowvec("gs", gs)
+        load_tab(0)
+        load_rowvec("sc", sc)
+        load_rowvec("gt", gt)
+        for q in range(QUADS):
+            nc.sync.dma_start(
+                tab_sc[32 * q : 32 * q + 4 * PASSES, :].bitcast(I32),
+                tab_scales[:, 4 * q : 4 * q + 4, :].bitcast(I32),
+            )
+        load_tab(1)
+        nc.sync.dma_start(w2_codes[:].bitcast(I32), w2_words.rearrange("a p c -> p a c").bitcast(I32))
+        for q in range(QUADS):
+            nc.sync.dma_start(
+                w2_sc[32 * q : 32 * q + 4, :, :].bitcast(I32),
+                w2_scales[:, 4 * q : 4 * q + 4, :].rearrange("a r c -> r a c").bitcast(I32),
+            )
+        load_tab(2)
+        load_rowvec("gv", gv)
+        nc.vector.tensor_copy(v_sc[0][:], tab_sc[:].indirect(idx[:]))
+        for a in range(1, PASSES):
+            nc.scalar.dma_start(v_sc[a][0:112, :].bitcast(I32), v_sc[0][4 * a : 4 * a + 112, :].bitcast(I32))
+        for a in range(PASSES):
+            nc.sync.dma_start(w1_raw[a][:], w1[a * 512 : (a + 1) * 512, :].rearrange("(p j) c -> p j c", j=PACK))
+
+        w4_raw = keep.tile([P, H], I32, name="w4_raw")
+        nc.sync.dma_start(w4_raw[:], w4_words[0].rearrange("p c i -> p (c i)").bitcast(I32))
+        for q in range(QUADS):
+            nc.sync.dma_start(
+                w4_sc_raw[32 * q : 32 * q + 4, :].bitcast(I32), w4_scales[0, 4 * q : 4 * q + 4, :].bitcast(I32)
+            )
 
         page = [keep.tile([P, T2], F32, name=f"page{t}") for t in range(PACK)]
         page_rows = page0.rearrange("(p t) c -> t p c", t=PACK)
@@ -115,8 +129,6 @@ def tile_list_handshape_page_features_kernel(
             for t in range(t0, t1):
                 gain[t, hf] = tile[:, t - t0, :]
 
-        nc.sync.dma_start(idx2[:], offs2)
-        load_rowvec("gs", gs)
         nc.sync.dma_start(page[0][:], page_rows[0])
         load_gain(0, 1, 0, 72 * KIB)
         nc.sync.dma_start(page[1][:], page_rows[1])
@@ -124,23 +136,8 @@ def tile_list_handshape_page_features_kernel(
         nc.sync.dma_start(page[2][:], page_rows[2])
         nc.sync.dma_start(page[3][:], page_rows[3])
         load_gain(0, PACK, 1, 80 * KIB)
-        nc.sync.dma_start(idx3[:], offs3)
-        load_rowvec("sc", sc)
-        load_rowvec("gt", gt)
         w3_raw = shared.tile([P, PACK, H], F32, name="w3_raw", offset=48 * KIB)
         nc.sync.dma_start(w3_raw[:], w3.rearrange("(p j) c -> p j c", j=PACK))
-        w4_codes = keep.tile([P, H], I32, name="w4_codes", align_bytes=64)
-        nc.sync.dma_start(w4_codes[:], w4_words[0].rearrange("p c i -> p (c i)").bitcast(I32))
-        for q in range(QUADS):
-            nc.sync.dma_start(
-                w4_sc[32 * q : 32 * q + 4, :].bitcast(I32), w4_scales[0, 4 * q : 4 * q + 4, :].bitcast(I32)
-            )
-        nc.sync.dma_start(idx4[:], offs4)
-        load_rowvec("gv", gv)
-
-        nc.vector.tensor_copy(v_sc[0][:], tab_sc[:].indirect(idx[:]))
-        for a in range(1, PASSES):
-            nc.scalar.dma_start(v_sc[a][0:112, :].bitcast(I32), v_sc[0][4 * a : 4 * a + 112, :].bitcast(I32))
 
         v = [keep.tile([P, S], U32, name=f"v{a}", align_bytes=64) for a in range(PASSES)]
         b_acc = [bank_tile(f"b_acc{jb}", jb) for jb in range(S // P)]
@@ -169,8 +166,8 @@ def tile_list_handshape_page_features_kernel(
             rounded = shared.tile([P, PACK, P], U32, name=f"rounded{jb}", offset=at[0])
             nc.scalar.activation(rounded[:], by_slot(b_acc[jb]), ACT.Copy, bias=ROUNDER, scale=1.0 / TWO_PI)
             turns[jb] = shared.tile([P, PACK, P], F32, name=f"turns{jb}", offset=at[1])
-            nc.scalar.activation(turns[jb][:], by_slot(b_acc[jb]), ACT.Copy, scale=1.0 / TWO_PI)
             whole[jb] = shared.tile([P, PACK, P], F32, name=f"whole{jb}", offset=at[2])
+            nc.scalar.activation(turns[jb][:], by_slot(b_acc[jb]), ACT.Copy, scale=1.0 / TWO_PI)
             nc.scalar.activation(whole[jb][:], rounded[:], ACT.Copy, bias=ROUNDER, scale=-1.0)
 
         def transpose_add(acc, first, second):
@@ -202,6 +199,15 @@ def tile_list_handshape_page_features_kernel(
             )
             w1_q.append(quantize_weight(grouped, f"w1_{a}"))
 
+        w4_codes = keep.tile([P, H], I32, name="w4_codes", align_bytes=64)
+        w4_sc = keep.tile([P, H], U8, name="w4_sc", align_bytes=64)
+        nc.vector.tensor_copy(
+            w4_codes[:].rearrange("p (t m) -> p m t", t=PACK), w4_raw[:].rearrange("p (m t) -> p m t", t=PACK)
+        )
+        nc.vector.tensor_copy(
+            w4_sc[:].rearrange("p (t m) -> p m t", t=PACK), w4_sc_raw[:].rearrange("p (m t) -> p m t", t=PACK)
+        )
+
         a_acc, entries = {}, {}
 
         def multiply_w1(t, hf):
@@ -232,8 +238,8 @@ def tile_list_handshape_page_features_kernel(
             )
 
         x = [shared.tile([P, 2, M], F32, name=f"x{u}", offset=32 * KIB + 8 * KIB * u) for u in range(2)]
-        t_in = [shared.tile([P, CHUNK, PACK], BF16, name=f"t_in{c}", offset=4 * KIB * c, align_bytes=64) for c in range(CHUNKS)]
-        e_in = [shared.tile([P, CHUNK, PACK], BF16, name=f"e_in{c}", offset=4 * KIB * c + 2 * KIB, align_bytes=64) for c in range(CHUNKS)]
+        t_in = [shared.tile([P, CHUNK, PACK], BF16, name=f"t_in{c}", offset=8 * KIB * c, align_bytes=64) for c in range(CHUNKS)]
+        e_in = [shared.tile([P, CHUNK, PACK], BF16, name=f"e_in{c}", offset=8 * KIB * c + 4 * KIB, align_bytes=64) for c in range(CHUNKS)]
 
         def reread(t, width):
             for part in range(M // width):
@@ -250,14 +256,14 @@ def tile_list_handshape_page_features_kernel(
         for hf in range(HALVES):
             for jb in range(hf * BLOCKS, (hf + 1) * BLOCKS):
                 split_turns(jb)
-            multiply_w1(0, hf)
-            multiply_w1(1, hf)
             for t in range(PACK):
+                if t < 2:
+                    multiply_w1(t, hf)
                 sine_of(t, hf)
         w3_grouped = ring.tile([P, PACK * H], BF16, name="grouped", align_bytes=64)
         nc.scalar.copy(
-            w3_grouped[:].rearrange("p (c i j) -> p c j i", i=PACK, j=PACK),
-            w3_raw[:].rearrange("p j (c i) -> p c j i", i=PACK),
+            w3_grouped[:].rearrange("p (t m j) -> p m j t", t=PACK, j=PACK),
+            w3_raw[:].rearrange("p j (m t) -> p m j t", t=PACK),
         )
 
         steps = [(t, hf) for hf in range(HALVES) for t in range(PACK)]
@@ -277,68 +283,58 @@ def tile_list_handshape_page_features_kernel(
             readings(PACK - 1, c)
 
         out_rows = out.rearrange("(p t) m -> p t m", t=PACK)
-        variants, staged, sums = {}, {}, {}
+        variants, sums = {}, {}
 
         def fetch_variants(c):
-            offset = 80 * KIB if c == 0 else 4 * KIB * (c - 1)
+            offset = 80 * KIB if c == 0 else 0
             variants[c] = shared.tile([P, PACK, CHUNK], F32, name=f"variants{c}", offset=offset)
             for t in range(PACK):
                 nc.vector.tensor_copy(variants[c][:, t, :], page[t][:].indirect(part_of_list(idx4, c, CHUNK)))
 
-        quantized = {}
-
-        def quantize_readings(c):
-            for name, src in (("t", t_in[c]), ("e", e_in[c])):
+        def second_stage(c):
+            for name, src in (("e", e_in[c]), ("t", t_in[c])):
                 codes = ring.tile([P, CHUNK], U32, name=name + "_codes", align_bytes=64)
                 scales = ring.tile([P, CHUNK], U8, name=name + "_sc", align_bytes=64)
                 nc.vector.quantize_mx(out=codes[:].bitcast(FP8X4), scales=scales[:], in_=src[:].rearrange("p m t -> p (m t)"))
                 quantized[c, name] = (codes, scales)
 
-        def multiply_block(mb):
-            c, i = divmod(mb, CHUNK // P)
-            for which, (name, w_codes, w_sc, sign) in enumerate((("t", w3_codes, w3_sc, 1.0), ("e", w4_codes, w4_sc, -1.0))):
-                codes, scales = quantized[c, name]
-                acc = bank_tile(f"y{mb}{name}", 2 * (mb % 2) + which)
+        def multiply(c, name, w_codes, w_sc, first_bank):
+            codes, scales = quantized[c, name]
+            for t in range(PACK):
+                sums[c, name, t] = bank_tile(f"y{name}{c}{t}", first_bank + t)
                 nc.tensor.matmul_mx(
-                    out=acc[:],
-                    lhsT=codes[:, span(i, P)].bitcast(FP8X4),
-                    lhsT_scale=scales[:, span(i, P)],
-                    rhs=w_codes[:].bitcast(FP8X4),
-                    rhs_scale=w_sc[:],
+                    out=sums[c, name, t][:],
+                    lhsT=w_codes[:, span(t, P)].bitcast(FP8X4),
+                    lhsT_scale=w_sc[:, span(t, P)],
+                    rhs=codes[:].bitcast(FP8X4),
+                    rhs_scale=scales[:],
                     start=True,
                     stop=True,
                 )
-                staged[mb, name] = shared.tile([P, PACK, P], F32, name=f"staged{mb}{name}", offset=(56 + 2 * (2 * (mb % 4) + which)) * KIB)
-                nc.scalar.activation(staged[mb, name][:], by_slot(acc), ACT.Copy, scale=sign)
-
-        def turn_back(mb):
-            c, i = divmod(mb, CHUNK // P)
-            if i == 0:
-                for u in range(2):
-                    sums[c, u] = psum.tile([P, 2, CHUNK], F32, name=f"sums{c}{u}", offset=(4 + 2 * (c % 2) + u) * BANK_BYTES)
-            for t in range(PACK):
-                transpose_add(sums[c, t // 2][:, t % 2, span(i, P)], staged[mb, "t"][:, t, :], staged[mb, "e"][:, t, :])
 
         def finish(c):
-            for u in range(2):
-                result = shared.tile([P, 2, CHUNK], F32, name=f"result{c}{u}", offset=16 * KIB + 2 * KIB * (2 * c + u))
-                for t in range(2 * u, 2 * u + 2):
-                    nc.vector.scalar_tensor_tensor(
-                        result[:, t % 2, :], variants[c][:, t, :], rowvec["gv"][:, t : t + 1], sums[c, u][:, t % 2, :], ALU.mult, ALU.add
-                    )
-                nc.sync.dma_start(out_rows[:, 2 * u : 2 * u + 2, span(c, CHUNK)], result[:])
+            multiply(c, "e", w4_codes, w4_sc, 0)
+            multiply(c, "t", w3_codes, w3_sc, PACK)
+            partial = []
+            for t in range(PACK):
+                part = shared.tile([P, CHUNK], F32, name=f"part{c}{t}", offset=(8 + 48 * c + 2 * t) * KIB)
+                nc.vector.scalar_tensor_tensor(
+                    part[:], variants[c][:, t, :], rowvec["gv"][:, t : t + 1], sums[c, "e", t][:], ALU.mult, ALU.subtract
+                )
+                partial.append(part)
+            for t in range(PACK):
+                result = shared.tile([P, CHUNK], F32, name=f"result{c}{t}", offset=16 * KIB + 2 * KIB * (4 * c + t))
+                if PACK * c + t < 5:
+                    staged = shared.tile([P, CHUNK], F32, name=f"staged{c}{t}", offset=(64 + 2 * t) * KIB)
+                    nc.scalar.copy(staged[:], sums[c, "t", t][:])
+                    nc.gpsimd.tensor_tensor(result[:], partial[t][:], staged[:], ALU.add)
+                else:
+                    nc.vector.tensor_tensor(result[:], partial[t][:], sums[c, "t", t][:], ALU.add)
+                nc.sync.dma_start(out_rows[:, t, span(c, CHUNK)], result[:])
 
-        blocks = M // P
-        for mb in range(blocks + 2):
-            c, i = divmod(mb, CHUNK // P)
-            if mb < blocks:
-                if i == 0:
-                    fetch_variants(c)
-                    quantize_readings(c)
-                multiply_block(mb)
-            if i == 0 and c >= 3:
-                finish(c - 3)
-            if mb >= 2:
-                turn_back(mb - 2)
-        finish(CHUNKS - 2)
-        finish(CHUNKS - 1)
+        quantized = {}
+        for c in range(CHUNKS):
+            fetch_variants(c)
+            second_stage(c)
+        for c in range(CHUNKS):
+            finish(c)

@@ -110,34 +110,31 @@ def tile_list_handshape_page_features_kernel(
         for a in range(PASSES):
             nc.sync.dma_start(w1_raw[a][:], w1[a * 512 : (a + 1) * 512, :].rearrange("(p j) c -> p j c", j=PACK))
 
+        page = [keep.tile([P, T2], F32, name=f"page{t}") for t in range(PACK)]
+        page_rows = page0.rearrange("(p t) c -> t p c", t=PACK)
+        gain_rows = wgs.rearrange("(m t) j -> m t j", t=PACK)
+        gain = {}
+
+        def load_gain(t0, t1, hf):
+            tile = shared.tile([P, t1 - t0, BANK], F32, name=f"gain{t0}{hf}", offset=(72 + 8 * hf + 2 * t0) * KIB)
+            for q in range(QUADS):
+                nc.sync.dma_start(tile[32 * q : 32 * (q + 1), :, :], gain_rows[:, t0:t1, span(hf, BANK)])
+            for t in range(t0, t1):
+                gain[t, hf] = tile[:, t - t0, :]
+
+        for t in range(PACK):
+            nc.sync.dma_start(page[t][:], page_rows[t])
+            load_gain(t, t + 1, 0)
+        load_gain(0, 2, 1)
+        w3_raw = shared.tile([P, PACK, H], F32, name="w3_raw", offset=48 * KIB)
+        nc.sync.dma_start(w3_raw[:], w3.rearrange("(p j) c -> p j c", j=PACK))
+        load_gain(2, PACK, 1)
         w4_raw = keep.tile([P, H], I32, name="w4_raw")
         nc.sync.dma_start(w4_raw[:], w4_words[0].rearrange("p c i -> p (c i)").bitcast(I32))
         for q in range(QUADS):
             nc.sync.dma_start(
                 w4_sc_raw[32 * q : 32 * q + 4, :].bitcast(I32), w4_scales[0, 4 * q : 4 * q + 4, :].bitcast(I32)
             )
-
-        page = [keep.tile([P, T2], F32, name=f"page{t}") for t in range(PACK)]
-        page_rows = page0.rearrange("(p t) c -> t p c", t=PACK)
-        gain_rows = wgs.rearrange("(m t) j -> m t j", t=PACK)
-        gain = {}
-
-        def load_gain(t0, t1, hf, offset):
-            tile = shared.tile([P, t1 - t0, BANK], F32, name=f"gain{t0}{hf}", offset=offset)
-            for q in range(QUADS):
-                nc.sync.dma_start(tile[32 * q : 32 * (q + 1), :, :], gain_rows[:, t0:t1, span(hf, BANK)])
-            for t in range(t0, t1):
-                gain[t, hf] = tile[:, t - t0, :]
-
-        nc.sync.dma_start(page[0][:], page_rows[0])
-        load_gain(0, 1, 0, 72 * KIB)
-        nc.sync.dma_start(page[1][:], page_rows[1])
-        load_gain(1, PACK, 0, 74 * KIB)
-        nc.sync.dma_start(page[2][:], page_rows[2])
-        nc.sync.dma_start(page[3][:], page_rows[3])
-        load_gain(0, PACK, 1, 80 * KIB)
-        w3_raw = shared.tile([P, PACK, H], F32, name="w3_raw", offset=48 * KIB)
-        nc.sync.dma_start(w3_raw[:], w3.rearrange("(p j) c -> p j c", j=PACK))
 
         v = [keep.tile([P, S], U32, name=f"v{a}", align_bytes=64) for a in range(PASSES)]
         b_acc = [bank_tile(f"b_acc{jb}", jb) for jb in range(S // P)]
@@ -199,15 +196,6 @@ def tile_list_handshape_page_features_kernel(
             )
             w1_q.append(quantize_weight(grouped, f"w1_{a}"))
 
-        w4_codes = keep.tile([P, H], I32, name="w4_codes", align_bytes=64)
-        w4_sc = keep.tile([P, H], U8, name="w4_sc", align_bytes=64)
-        nc.vector.tensor_copy(
-            w4_codes[:].rearrange("p (t m) -> p m t", t=PACK), w4_raw[:].rearrange("p (m t) -> p m t", t=PACK)
-        )
-        nc.vector.tensor_copy(
-            w4_sc[:].rearrange("p (t m) -> p m t", t=PACK), w4_sc_raw[:].rearrange("p (m t) -> p m t", t=PACK)
-        )
-
         a_acc, entries = {}, {}
 
         def multiply_w1(t, hf):
@@ -245,20 +233,34 @@ def tile_list_handshape_page_features_kernel(
             for part in range(M // width):
                 nc.vector.tensor_copy(x[t // 2][:, t % 2, span(part, width)], page[t][:].indirect(part_of_list(idx3, part, width)))
 
-        def readings(t, c):
-            cols = span(c, CHUNK)
-            if t % 2 == 1:
-                nc.scalar.activation(e_in[c][:, :, t - 1 : t + 1], x[t // 2][:, :, cols].rearrange("p u m -> p m u"), ACT.Abs)
-            bounded = ring.tile([P, CHUNK], F32, name="bounded")
-            nc.scalar.activation(bounded[:], x[t // 2][:, t % 2, cols], ACT.Tanh, scale=rowvec["sc"][:, t : t + 1])
-            nc.scalar.activation(t_in[c][:, :, t], bounded[:], ACT.Copy, scale=rowvec["gt"][:, t : t + 1])
+        def readings(t):
+            bounded = [ring.tile([P, CHUNK], F32, name="bounded", bufs=4) for c in range(CHUNKS)]
+
+            def squash(c):
+                nc.scalar.activation(bounded[c][:], x[t // 2][:, t % 2, span(c, CHUNK)], ACT.Tanh, scale=rowvec["sc"][:, t : t + 1])
+
+            def weigh(c):
+                nc.scalar.activation(t_in[c][:, :, t], bounded[c][:], ACT.Copy, scale=rowvec["gt"][:, t : t + 1])
+
+            def magnitudes(c):
+                pair = x[t // 2][:, :, span(c, CHUNK)].rearrange("p u m -> p m u")
+                nc.scalar.activation(e_in[c][:, :, t - 1 : t + 1], pair, ACT.Abs)
+
+            if t % 2 == 0:
+                for step in (squash, weigh):
+                    for c in range(CHUNKS):
+                        step(c)
+            else:
+                for c in range(CHUNKS):
+                    for step in (squash, magnitudes, weigh):
+                        step(c)
 
         for hf in range(HALVES):
             for jb in range(hf * BLOCKS, (hf + 1) * BLOCKS):
                 split_turns(jb)
+            multiply_w1(0, hf)
+            multiply_w1(1, hf)
             for t in range(PACK):
-                if t < 2:
-                    multiply_w1(t, hf)
                 sine_of(t, hf)
         w3_grouped = ring.tile([P, PACK * H], BF16, name="grouped", align_bytes=64)
         nc.scalar.copy(
@@ -273,23 +275,30 @@ def tile_list_handshape_page_features_kernel(
                 make_entries(*steps[i + 1])
             else:
                 w3_codes, w3_sc = quantize_weight(w3_grouped, "w3")
+                w4_codes = keep.tile([P, H], I32, name="w4_codes", align_bytes=64)
+                w4_sc = keep.tile([P, H], U8, name="w4_sc", align_bytes=64)
+                nc.vector.tensor_copy(
+                    w4_codes[:].rearrange("p (t m) -> p m t", t=PACK), w4_raw[:].rearrange("p (m t) -> p m t", t=PACK)
+                )
+                nc.vector.tensor_copy(
+                    w4_sc[:].rearrange("p (t m) -> p m t", t=PACK), w4_sc_raw[:].rearrange("p (m t) -> p m t", t=PACK)
+                )
             put_entries(t, hf)
             if hf == HALVES - 1 and t < PACK - 1:
                 reread(t, M)
-                for c in range(CHUNKS):
-                    readings(t, c)
+                readings(t)
         reread(PACK - 1, CHUNK)
-        for c in range(CHUNKS):
-            readings(PACK - 1, c)
+        readings(PACK - 1)
 
         out_rows = out.rearrange("(p t) m -> p t m", t=PACK)
         variants, sums = {}, {}
 
         def fetch_variants(c):
             offset = 80 * KIB if c == 0 else 0
-            variants[c] = shared.tile([P, PACK, CHUNK], F32, name=f"variants{c}", offset=offset)
+            tile = shared.tile([P, PACK, CHUNK], F32, name=f"variants{c}", offset=offset)
             for t in range(PACK):
-                nc.vector.tensor_copy(variants[c][:, t, :], page[t][:].indirect(part_of_list(idx4, c, CHUNK)))
+                variants[c, t] = tile[:, t, :]
+                nc.vector.tensor_copy(variants[c, t], page[t][:].indirect(part_of_list(idx4, c, CHUNK)))
 
         def second_stage(c):
             for name, src in (("e", e_in[c]), ("t", t_in[c])):
@@ -313,18 +322,18 @@ def tile_list_handshape_page_features_kernel(
                 )
 
         def finish(c):
-            multiply(c, "e", w4_codes, w4_sc, 0)
             multiply(c, "t", w3_codes, w3_sc, PACK)
+            multiply(c, "e", w4_codes, w4_sc, 0)
             partial = []
             for t in range(PACK):
                 part = shared.tile([P, CHUNK], F32, name=f"part{c}{t}", offset=(8 + 48 * c + 2 * t) * KIB)
                 nc.vector.scalar_tensor_tensor(
-                    part[:], variants[c][:, t, :], rowvec["gv"][:, t : t + 1], sums[c, "e", t][:], ALU.mult, ALU.subtract
+                    part[:], variants[c, t], rowvec["gv"][:, t : t + 1], sums[c, "e", t][:], ALU.mult, ALU.subtract
                 )
                 partial.append(part)
             for t in range(PACK):
                 result = shared.tile([P, CHUNK], F32, name=f"result{c}{t}", offset=16 * KIB + 2 * KIB * (4 * c + t))
-                if PACK * c + t < 5:
+                if PACK * c + t < 4:
                     staged = shared.tile([P, CHUNK], F32, name=f"staged{c}{t}", offset=(64 + 2 * t) * KIB)
                     nc.scalar.copy(staged[:], sums[c, "t", t][:])
                     nc.gpsimd.tensor_tensor(result[:], partial[t][:], staged[:], ALU.add)

import math
from contextlib import ExitStack

import concourse.mybir as mybir
from concourse.masks import make_identity

K, H, T, S, T2, M = 1536, 512, 4096, 1024, 2048, 1024
FLOPS = 2 * (2 * K * H * S) + 2 * (2 * H * H * M)

F32 = mybir.dt.float32
BF16 = mybir.dt.bfloat16
I32 = mybir.dt.int32
U32 = mybir.dt.uint32
U16 = mybir.dt.uint16
U8 = mybir.dt.uint8
FP8X4 = mybir.dt.float8_e4m3fn_x4
FP4X4 = mybir.dt.float4_e2m1fn_x4
ALU = mybir.AluOpType
ACT = mybir.ActivationFunctionType

P = 128
PACK = 4
PASSES = K // (P * PACK)
BANK = 512
BANK_BYTES = 4 * BANK
HALVES = S // BANK
BLOCKS = BANK // P
CHUNK = 512
CHUNKS = M // CHUNK
QUADS = 4
TWO_PI = 2.0 * math.pi
ROUNDER = 1.5 * 2.0**23
KIB = 1024


def tile_list_handshape_page_features_kernel(
    tc, tab_words, tab_scales, offs, offs2, offs3, offs4, w1, w2_words, w2_scales, gs, wgs, page0, sc, gt, w3,
    w4_words, w4_scales, gv, out,
):
    nc = tc.nc
    with ExitStack() as ctx:
        lists = ctx.enter_context(tc.tile_pool(name="lists", bufs=1))
        keep = ctx.enter_context(tc.tile_pool(name="keep", bufs=1))
        shared = ctx.enter_context(tc.tile_pool(name="shared", bufs=1))
        ring = ctx.enter_context(tc.tile_pool(name="ring", bufs=2))
        psum = ctx.enter_context(tc.psum_pool(name="psum", bufs=1))

        def part_of_list(tile, part, width):
            cols = width // 16
            return tile[:, part * cols : (part + 1) * cols]

        def span(part, width):
            return slice(part * width, (part + 1) * width)

        def bank_tile(name, bank):
            return psum.tile([P, BANK], F32, name=name, offset=bank * BANK_BYTES)

        idx = lists.tile([P, S // 16], U16, name="idx")
        idx2 = lists.tile([P, S // 16], U16, name="idx2")
        idx3 = lists.tile([P, M // 16], U16, name="idx3")
        idx4 = lists.tile([P, M // 16], U16, name="idx4")

        tab = [shared.tile([P, T], I32, name=f"tab{a}", offset=16 * KIB * a) for a in range(PASSES)]
        w1_raw = [shared.tile([P, PACK, H], F32, name=f"w1_raw{a}", offset=48 * KIB + 8 * KIB * a) for a in range(PASSES)]

        tab_sc = keep.tile([P, T], U8, name="tab_sc")
        v_sc = [keep.tile([P, S], U8, name=f"v_sc{a}", align_bytes=64) for a in range(PASSES)]
        w2_codes = keep.tile([P, PASSES, 2 * H], U8, name="w2_codes", align_bytes=64)
        w2_sc = keep.tile([P, PASSES, H], U8, name="w2_sc", align_bytes=64)
        w4_sc_raw = keep.tile([P, H], U8, name="w4_sc_raw")
        for tile in (tab_sc[:], w2_sc[:].rearrange("p a c -> p (a c)"), v_sc[1][:], v_sc[2][:], w4_sc_raw[:]):
            nc.vector.memset(tile.bitcast(I32), 0)
        ident = keep.tile([P, P], F32, name="ident")
        make_identity(nc, ident[:])
        warm = keep.tile([P, 1], F32, name="warm")
        nc.scalar.activation(warm[:], ident[:, 0:1], ACT.Silu)

        rowvec = {}

        def load_rowvec(name, vec):
            rowvec[name] = keep.tile([P, PACK], F32, name=name)
            nc.sync.dma_start(rowvec[name][:], vec.rearrange("(p t) -> p t", t=PACK))

        def load_tab(a):
            nc.sync.dma_start(tab[a][:], tab_words[a].rearrange("p t i -> p (t i)").bitcast(I32))

        for tile, src in ((idx, offs), (idx2, offs2), (idx3, offs3), (idx4, offs4)):
            nc.sync.dma_start(tile[:], src)
        load_rowvec("gs", gs)
        load_tab(0)
        load_rowvec("sc", sc)
        load_rowvec("gt", gt)
        for q in range(QUADS):
            nc.sync.dma_start(
                tab_sc[32 * q : 32 * q + 4 * PASSES, :].bitcast(I32),
                tab_scales[:, 4 * q : 4 * q + 4, :].bitcast(I32),
            )
        load_tab(1)
        nc.sync.dma_start(w2_codes[:].bitcast(I32), w2_words.rearrange("a p c -> p a c").bitcast(I32))
        for q in range(QUADS):
            nc.sync.dma_start(
                w2_sc[32 * q : 32 * q + 4, :, :].bitcast(I32),
                w2_scales[:, 4 * q : 4 * q + 4, :].rearrange("a r c -> r a c").bitcast(I32),
            )
        load_tab(2)
        load_rowvec("gv", gv)
        nc.vector.tensor_copy(v_sc[0][:], tab_sc[:].indirect(idx[:]))
        for a in range(1, PASSES):
            nc.scalar.dma_start(v_sc[a][0:112, :].bitcast(I32), v_sc[0][4 * a : 4 * a + 112, :].bitcast(I32))
        for a in range(PASSES):
            nc.sync.dma_start(w1_raw[a][:], w1[a * 512 : (a + 1) * 512, :].rearrange("(p j) c -> p j c", j=PACK))

        page = [keep.tile([P, T2], F32, name=f"page{t}") for t in range(PACK)]
        page_rows = page0.rearrange("(p t) c -> t p c", t=PACK)
        gain_rows = wgs.rearrange("(m t) j -> m t j", t=PACK)
        gain = {}

        def load_gain(t0, t1, hf):
            tile = shared.tile([P, t1 - t0, BANK], F32, name=f"gain{t0}{hf}", offset=(72 + 8 * hf + 2 * t0) * KIB)
            for q in range(QUADS):
                nc.sync.dma_start(tile[32 * q : 32 * (q + 1), :, :], gain_rows[:, t0:t1, span(hf, BANK)])
            for t in range(t0, t1):
                gain[t, hf] = tile[:, t - t0, :]

        for t in range(PACK):
            nc.sync.dma_start(page[t][:], page_rows[t])
            load_gain(t, t + 1, 0)
        load_gain(0, 2, 1)
        w3_raw = shared.tile([P, PACK, H], F32, name="w3_raw", offset=48 * KIB)
        nc.sync.dma_start(w3_raw[:], w3.rearrange("(p j) c -> p j c", j=PACK))
        load_gain(2, PACK, 1)
        w4_raw = keep.tile([P, H], I32, name="w4_raw")
        nc.sync.dma_start(w4_raw[:], w4_words[0].rearrange("p c i -> p (c i)").bitcast(I32))
        for q in range(QUADS):
            nc.sync.dma_start(
                w4_sc_raw[32 * q : 32 * q + 4, :].bitcast(I32), w4_scales[0, 4 * q : 4 * q + 4, :].bitcast(I32)
            )

        v = [keep.tile([P, S], U32, name=f"v{a}", align_bytes=64) for a in range(PASSES)]
        b_acc = [bank_tile(f"b_acc{jb}", jb) for jb in range(S // P)]
        for a in range(PASSES):
            for hf in range(HALVES):
                nc.vector.tensor_copy(v[a][:, span(hf, BANK)], tab[a][:].bitcast(U32).indirect(part_of_list(idx, hf, BANK)))
                for jb in range(hf * BLOCKS, (hf + 1) * BLOCKS):
                    nc.tensor.matmul_mx(
                        out=b_acc[jb][:],
                        lhsT=v[a][:, span(jb, P)].bitcast(FP8X4),
                        lhsT_scale=v_sc[a][:, span(jb, P)],
                        rhs=w2_codes[:, a, :].bitcast(FP4X4),
                        rhs_scale=w2_sc[:, a, :],
                        start=(a == 0),
                        stop=(a == PASSES - 1),
                    )

        def by_slot(acc):
            return acc[:].rearrange("p (m t) -> p t m", t=PACK)

        turns, whole = {}, {}

        def split_turns(jb):
            hf, i = divmod(jb, BLOCKS)
            at = [8 * KIB * ((k + hf) % 3) + 2 * KIB * i for k in range(3)]
            rounded = shared.tile([P, PACK, P], U32, name=f"rounded{jb}", offset=at[0])
            nc.scalar.activation(rounded[:], by_slot(b_acc[jb]), ACT.Copy, bias=ROUNDER, scale=1.0 / TWO_PI)
            turns[jb] = shared.tile([P, PACK, P], F32, name=f"turns{jb}", offset=at[1])
            whole[jb] = shared.tile([P, PACK, P], F32, name=f"whole{jb}", offset=at[2])
            nc.scalar.activation(turns[jb][:], by_slot(b_acc[jb]), ACT.Copy, scale=1.0 / TWO_PI)
            nc.scalar.activation(whole[jb][:], rounded[:], ACT.Copy, bias=ROUNDER, scale=-1.0)

        def transpose_add(acc, first, second):
            nc.tensor.matmul(acc, first, ident[:], is_transpose=True, start=True, stop=False)
            nc.tensor.matmul(acc, second, ident[:], is_transpose=True, start=False, stop=True)

        sine = {}

        def sine_of(t, hf):
            frac = bank_tile(f"frac{t}{hf}", 4 * hf + 2 + t % 2)
            for i in range(BLOCKS):
                jb = hf * BLOCKS + i
                transpose_add(frac[:, span(i, P)], turns[jb][:, t, :], whole[jb][:, t, :])
            sine[t, hf] = keep.tile([P, BANK], F32, name=f"sine{t}{hf}")
            nc.scalar.activation(sine[t, hf][:], frac[:], ACT.Sin, scale=TWO_PI)

        def quantize_weight(grouped, name):
            codes = keep.tile([P, H], U32, name=name + "_codes", align_bytes=64)
            scales = keep.tile([P, H], U8, name=name + "_sc", align_bytes=64)
            nc.vector.quantize_mx(out=codes[:].bitcast(FP8X4), scales=scales[:], in_=grouped[:])
            return codes, scales

        w1_q = []
        for a in range(PASSES):
            grouped = ring.tile([P, PACK * H], BF16, name="grouped", align_bytes=64)
            nc.vector.tensor_copy(
                grouped[:].rearrange("p (t m j) -> p m j t", t=PACK, j=PACK),
                w1_raw[a][:].rearrange("p j (m t) -> p m j t", t=PACK),
            )
            w1_q.append(quantize_weight(grouped, f"w1_{a}"))

        a_acc, entries = {}, {}

        def multiply_w1(t, hf):
            acc = bank_tile(f"a_acc{t}{hf}", 4 * hf + t % 2)
            for a in range(PASSES):
                nc.tensor.matmul_mx(
                    out=acc[:],
                    lhsT=w1_q[a][0][:, span(t, P)].bitcast(FP8X4),
                    lhsT_scale=w1_q[a][1][:, span(t, P)],
                    rhs=v[a][:, span(hf, BANK)].bitcast(FP8X4),
                    rhs_scale=v_sc[0][4 * a : P, span(hf, BANK)],
                    start=(a == 0),
                    stop=(a == PASSES - 1),
                )
            a_acc[t, hf] = acc

        def make_entries(t, hf):
            entries[t, hf] = ring.tile([P, BANK], F32, name="entries", bufs=3)
            nc.vector.scalar_tensor_tensor(
                entries[t, hf][:], sine[t, hf][:], rowvec["gs"][:, t : t + 1], a_acc[t, hf][:], ALU.mult, ALU.add
            )
            if t + 2 < PACK:
                multiply_w1(t + 2, hf)

        def put_entries(t, hf):
            nc.vector.tensor_tensor(
                page[t][:].indirect(part_of_list(idx2, hf, BANK)), entries[t, hf][:], gain[t, hf], ALU.mult
            )

        x = [shared.tile([P, 2, M], F32, name=f"x{u}", offset=32 * KIB + 8 * KIB * u) for u in range(2)]
        t_in = [shared.tile([P, CHUNK, PACK], BF16, name=f"t_in{c}", offset=8 * KIB * c, align_bytes=64) for c in range(CHUNKS)]
        e_in = [shared.tile([P, CHUNK, PACK], BF16, name=f"e_in{c}", offset=8 * KIB * c + 4 * KIB, align_bytes=64) for c in range(CHUNKS)]

        def reread(t, width):
            for part in range(M // width):
                nc.vector.tensor_copy(x[t // 2][:, t % 2, span(part, width)], page[t][:].indirect(part_of_list(idx3, part, width)))

        def readings(t):
            bounded = [ring.tile([P, CHUNK], F32, name="bounded", bufs=4) for c in range(CHUNKS)]

            def squash(c):
                nc.scalar.activation(bounded[c][:], x[t // 2][:, t % 2, span(c, CHUNK)], ACT.Tanh, scale=rowvec["sc"][:, t : t + 1])

            def weigh(c):
                nc.scalar.activation(t_in[c][:, :, t], bounded[c][:], ACT.Copy, scale=rowvec["gt"][:, t : t + 1])

            def magnitudes(c):
                pair = x[t // 2][:, :, span(c, CHUNK)].rearrange("p u m -> p m u")
                nc.scalar.activation(e_in[c][:, :, t - 1 : t + 1], pair, ACT.Abs)

            if t % 2 == 0:
                for step in (squash, weigh):
                    for c in range(CHUNKS):
                        step(c)
            else:
                for c in range(CHUNKS):
                    for step in (squash, magnitudes, weigh):
                        step(c)

        for hf in range(HALVES):
            for jb in range(hf * BLOCKS, (hf + 1) * BLOCKS):
                split_turns(jb)
            multiply_w1(0, hf)
            multiply_w1(1, hf)
            for t in range(PACK):
                sine_of(t, hf)
        w3_grouped = ring.tile([P, PACK * H], BF16, name="grouped", align_bytes=64)
        nc.scalar.copy(
            w3_grouped[:].rearrange("p (t m j) -> p m j t", t=PACK, j=PACK),
            w3_raw[:].rearrange("p j (m t) -> p m j t", t=PACK),
        )

        steps = [(t, hf) for hf in range(HALVES) for t in range(PACK)]
        make_entries(*steps[0])
        for i, (t, hf) in enumerate(steps):
            if i + 1 < len(steps):
                make_entries(*steps[i + 1])
            else:
                w3_codes, w3_sc = quantize_weight(w3_grouped, "w3")
                w4_codes = keep.tile([P, H], I32, name="w4_codes", align_bytes=64)
                w4_sc = keep.tile([P, H], U8, name="w4_sc", align_bytes=64)
                nc.vector.tensor_copy(
                    w4_codes[:].rearrange("p (t m) -> p m t", t=PACK), w4_raw[:].rearrange("p (m t) -> p m t", t=PACK)
                )
                nc.vector.tensor_copy(
                    w4_sc[:].rearrange("p (t m) -> p m t", t=PACK), w4_sc_raw[:].rearrange("p (m t) -> p m t", t=PACK)
                )
            put_entries(t, hf)
            if hf == HALVES - 1 and t < PACK - 1:
                reread(t, M)
                readings(t)
        reread(PACK - 1, CHUNK)
        readings(PACK - 1)

        out_rows = out.rearrange("(p t) m -> p t m", t=PACK)
        variants, sums = {}, {}

        def fetch_variants(c):
            offset = 80 * KIB if c == 0 else 0
            tile = shared.tile([P, PACK, CHUNK], F32, name=f"variants{c}", offset=offset)
            for t in range(PACK):
                variants[c, t] = tile[:, t, :]
                nc.vector.tensor_copy(variants[c, t], page[t][:].indirect(part_of_list(idx4, c, CHUNK)))

        def second_stage(c):
            for name, src in (("e", e_in[c]), ("t", t_in[c])):
                codes = ring.tile([P, CHUNK], U32, name=name + "_codes", align_bytes=64)
                scales = ring.tile([P, CHUNK], U8, name=name + "_sc", align_bytes=64)
                nc.vector.quantize_mx(out=codes[:].bitcast(FP8X4), scales=scales[:], in_=src[:].rearrange("p m t -> p (m t)"))
                quantized[c, name] = (codes, scales)

        def multiply(c, name, w_codes, w_sc, first_bank):
            codes, scales = quantized[c, name]
            for t in range(PACK):
                sums[c, name, t] = bank_tile(f"y{name}{c}{t}", first_bank + t)
                nc.tensor.matmul_mx(
                    out=sums[c, name, t][:],
                    lhsT=w_codes[:, span(t, P)].bitcast(FP8X4),
                    lhsT_scale=w_sc[:, span(t, P)],
                    rhs=codes[:].bitcast(FP8X4),
                    rhs_scale=scales[:],
                    start=True,
                    stop=True,
                )

        def finish(c):
            multiply(c, "t", w3_codes, w3_sc, PACK)
            multiply(c, "e", w4_codes, w4_sc, 0)
            partial = []
            for t in range(PACK):
                part = shared.tile([P, CHUNK], F32, name=f"part{c}{t}", offset=(8 + 48 * c + 2 * t) * KIB)
                nc.vector.scalar_tensor_tensor(
                    part[:], variants[c, t], rowvec["gv"][:, t : t + 1], sums[c, "e", t][:], ALU.mult, ALU.subtract
                )
                partial.append(part)
            for t in range(PACK):
                result = shared.tile([P, CHUNK], F32, name=f"result{c}{t}", offset=16 * KIB + 2 * KIB * (4 * c + t))
                if PACK * c + t < 4:
                    staged = shared.tile([P, CHUNK], F32, name=f"staged{c}{t}", offset=(64 + 2 * t) * KIB)
                    nc.scalar.copy(staged[:], sums[c, "t", t][:])
                    nc.gpsimd.tensor_tensor(result[:], partial[t][:], staged[:], ALU.add)
                else:
                    nc.vector.tensor_tensor(result[:], partial[t][:], sums[c, "t", t][:], ALU.add)
                nc.sync.dma_start(out_rows[:, t, span(c, CHUNK)], result[:])

        quantized = {}
        for c in range(CHUNKS):
            fetch_variants(c)
            second_stage(c)
        for c in range(CHUNKS):
            finish(c)
